import numpy as np
import ml_dtypes


def mxq(x, axis, fmt="e4m3"):
    dtype, down = {"e4m3": (ml_dtypes.float8_e4m3fn, 7), "e5m2": (ml_dtypes.float8_e5m2, 14)}[fmt]
    v = np.moveaxis(np.asarray(x, np.float32).astype(ml_dtypes.bfloat16).astype(np.float64), axis, -1)
    blocks = v.reshape(v.shape[:-1] + (-1, 32))
    amax = np.abs(blocks).max(-1, keepdims=True)
    byte = np.maximum(np.where(amax > 0, np.frexp(amax)[1] - 1 + 127, 0) - down, 1)
    scale = np.exp2(byte - 127.0)
    codes = (blocks / scale).astype(np.float32).astype(dtype).astype(np.float64)
    return np.moveaxis((codes * scale).reshape(v.shape), -1, axis)


WIDE = False


def mx_kscale(k):
    if not WIDE:
        return np.ones(k)
    levels = np.array([10, -10, 5, -5, 0])
    if k % 512:
        return np.exp2(np.random.permutation(np.resize(levels, k // 32))).repeat(32)
    a = np.empty((k // 512, 16))
    for p in range(k // 512):
        a[p, :8] = np.random.permutation(np.resize(levels, 8))
        for g in range(8):
            far = levels[np.abs(levels - a[p, g]) >= 10]
            a[p, g + 8] = far[np.random.randint(len(far))]
    return np.exp2(a.ravel()).repeat(32)


BF16 = ml_dtypes.bfloat16


def bf(x):
    return np.asarray(x, np.float32).astype(BF16)


def f64(x):
    return np.asarray(x).astype(np.float64)


E2M1 = np.array([0.0, 0.5, 1.0, 1.5, 2.0, 3.0, 4.0, 6.0, -0.0, -0.5, -1.0, -1.5, -2.0, -3.0, -4.0, -6.0])


def pack_weight(w, fmt):
    k, n = w.shape
    w = f64(bf(w)).reshape(k // 32, 32, n)
    amax = np.abs(w).max(1)
    if fmt == "e4m3":
        byte = np.frexp(amax)[1] - 1 + 127 - 7
    else:
        mant, ex = np.frexp(amax / 6.0)
        byte = np.where(mant > 0.5, ex, ex - 1) + 127
    byte = np.clip(np.where(amax > 0, byte, 1), 1, 254)
    scaled = (w * np.exp2(127.0 - byte)[:, None, :]).reshape(k, n).astype(np.float32)
    by_word = np.ascontiguousarray(scaled.reshape(k // 512, 128, 4, n).transpose(0, 1, 3, 2))
    if fmt == "e4m3":
        words = by_word.astype(ml_dtypes.float8_e4m3fn).view(np.uint8)
    else:
        c = by_word.astype(ml_dtypes.float4_e2m1fn).view(np.uint8) & 0xF
        words = c[..., 0::2] | (c[..., 1::2] << 4)
    return np.ascontiguousarray(words), np.ascontiguousarray(byte.astype(np.uint8).reshape(k // 512, 16, n))


def unpack_weight(words, scales, fmt):
    g, p, n, _ = words.shape
    if fmt == "e4m3":
        vals = np.ascontiguousarray(words).view(ml_dtypes.float8_e4m3fn).astype(np.float64)
    else:
        nib = np.empty((g, p, n, 4), np.uint8)
        nib[..., 0::2] = words & 0xF
        nib[..., 1::2] = words >> 4
        vals = E2M1[nib]
    vals = vals * np.repeat(np.exp2(scales.astype(np.float64) - 127.0), 8, axis=1)[..., None]
    return vals.transpose(0, 1, 3, 2).reshape(g * 512, n)
def pack4(w):
    words, scales = pack_weight(w, "e2m1")
    return words.reshape(words.shape[0], 128, -1), scales


def unpack4(words, scales):
    return unpack_weight(words.reshape(words.shape[0], 128, -1, 2), scales, "e2m1")


def planes(Y):
    n, m = Y.shape
    b = f64(bf(Y)).reshape(n // 32, 32, m)
    amax = np.abs(b).max(1)
    byte = np.clip(np.where(amax > 0, np.frexp(amax)[1] - 1 + 127 - 7, 1), 1, 254)
    codes = (b * np.exp2(127.0 - byte)[:, None, :]).reshape(n, m).astype(np.float32).astype(ml_dtypes.float8_e4m3fn).view(np.uint8)
    words = codes.reshape(n // 512, 128, 4, m).transpose(0, 1, 3, 2)
    return np.ascontiguousarray(words), np.ascontiguousarray(byte.astype(np.uint8).reshape(n // 512, 16, m))


B, N, D, F, G, C = 4, 64, 2048, 512, 512, 3
F2 = 2 * F


def _sigmoid(y):
    return 1.0 / (1.0 + np.exp(-y))


def _silu(y):
    return y * _sigmoid(y)


def _pair_sq_dist(pos):
    diff = pos[:, :, None, :] - pos[:, None, :, :]
    return np.sum(diff * diff, axis=-1)


def setup_inputs():
    s, t = mx_kscale(D), mx_kscale(F)
    h = bf(np.random.standard_normal((B, N, D)) * s)
    pos = bf(np.random.standard_normal((B, N, C)))
    w1_words, w1_scales = pack4(np.random.standard_normal((D, F2)) / np.sqrt(D) / s[:, None])
    wr = bf(np.random.standard_normal(F) * 0.2)
    edge_gain = bf((1.0 + 0.1 * np.random.standard_normal(F)) * t)
    w2_words, w2_scales = pack4(np.random.standard_normal((F, G)) / np.sqrt(F) / t[:, None])
    gate_w = bf(np.random.standard_normal(G) / np.sqrt(G))
    return {
        "h": h,
        "pos": pos,
        "w1_words": w1_words,
        "w1_scales": w1_scales,
        "wr": wr,
        "edge_gain": edge_gain,
        "w2_words": w2_words,
        "w2_scales": w2_scales,
        "gate_w": gate_w,
    }


def core(h, pos, w1_words, w1_scales, wr, edge_gain, w2_words, w2_scales, gate_w):
    w2 = unpack4(w2_words, w2_scales)
    b, n, _ = h.shape
    f = w2.shape[0]

    uv = mxq(f64(h), 2, "e4m3") @ unpack4(w1_words, w1_scales)
    u = uv[..., :f]
    v = uv[..., f:]

    r2 = _pair_sq_dist(f64(pos))

    pre = u[:, :, None, :] + v[:, None, :, :] + r2[..., None] * f64(wr)

    a = _silu(pre) * f64(edge_gain)

    rows = a.reshape(b * n * n, f)
    m = _silu(mxq(rows, 1, "e4m3") @ w2).reshape(b, n, n, w2.shape[1])

    g = _sigmoid(np.sum(m * f64(gate_w), axis=-1))

    return np.sum(g[..., None] * m, axis=2) / np.sqrt(n)


def reference(h, pos, w1_words, w1_scales, wr, edge_gain, w2_words, w2_scales, gate_w):
    R_out = core(h, pos, w1_words, w1_scales, wr, edge_gain, w2_words, w2_scales, gate_w)
    words, scales = planes(np.moveaxis(R_out, 2, 0).reshape(512, -1))
    return R_out, words, scales

@@ -1,0 +1,385 @@
+from contextlib import ExitStack
+
+import concourse.mybir as mybir
+from concourse.masks import make_identity
+
+F32 = mybir.dt.float32
+BF16 = mybir.dt.bfloat16
+I32 = mybir.dt.int32
+U32 = mybir.dt.uint32
+U8 = mybir.dt.uint8
+FP8X4 = mybir.dt.float8_e4m3fn_x4
+FP4X4 = mybir.dt.float4_e2m1fn_x4
+ACT = mybir.ActivationFunctionType
+ALU = mybir.AluOpType
+
+P = 128
+B, N, D, F = 4, 64, 2048, 512
+GROUPS = D // 512
+TOK = B * N
+HALF = 128
+IB = 8
+ROWS = IB * N
+BLOCKS = TOK // IB
+TILES = ROWS // P
+FLOPS = 2 * TOK * D * 2 * F + 2 * B * N * N * F * F
+
+
+def tile_egnngatededgelayer_x2_kernel(
+    tc, h, pos, w1_words, w1_scales, wr, edge_gain, w2_words, w2_scales, gate_w, out_0, out_1, out_2
+):
+    nc = tc.nc
+    with ExitStack() as ctx:
+        const = ctx.enter_context(tc.tile_pool(name="const", bufs=1))
+        work = ctx.enter_context(tc.tile_pool(name="work", bufs=3))
+        msgs = ctx.enter_context(tc.tile_pool(name="msgs", bufs=12))
+        psum = ctx.enter_context(tc.psum_pool(name="psum", bufs=1))
+        ctx.enter_context(tc.manual_schedule())
+
+        def bank(name):
+            return psum.tile([P, 512], F32, name=name, tag="mm", bufs=4)
+
+        w1s = const.tile([P, GROUPS, 2 * F], U8, name="w1s", align_bytes=64)
+        w1s_i = w1s[:].rearrange("p g n -> p (g n)").bitcast(I32).rearrange("p (g n) -> p g n", g=GROUPS)
+        w2s_raw = const.tile([P, F], U8, name="w2s_raw", align_bytes=64)
+        pos4 = const.tile([P, N * 3], BF16, name="pos4")
+        pos32 = const.tile([P, IB * 3], BF16, name="pos32")
+        gate_row = const.tile([P, F], BF16, name="gate_row")
+        gate_perm = const.tile([P, F], BF16, name="gate_perm")
+        ones = const.tile([P, P], BF16, name="ones")
+        ident = const.tile([P, P], F32, name="ident")
+        mask = const.tile([P, 2], F32, name="mask")
+        wr_raw = const.tile([P, 4], BF16, name="wr_raw")
+        gain_raw = const.tile([P, 4], BF16, name="gain_raw")
+        wg = const.tile([P, 2, 4], F32, name="wg")
+
+        nc.vector.memset(pos4[:], 0.0)
+        nc.vector.memset(pos32[:], 0.0)
+        make_identity(nc, ident[:])
+        nc.vector.memset(w1s[:].rearrange("p g n -> p (g n)").bitcast(I32), 0)
+        nc.gpsimd.memset(gate_row[:], 0.0)
+        nc.gpsimd.memset(w2s_raw[:].bitcast(I32), 0)
+        nc.gpsimd.memset(ones[:], 1.0)
+        for s in range(2):
+            for v in range(2):
+                nc.gpsimd.memset(mask[64 * v : 64 * v + 64, s : s + 1], 0.0625 if s == v else 0.0)
+
+        h_flat = h.rearrange("b n d -> (b n) d")
+        h_sb = [const.tile([P, D], BF16, name="h_sb%d" % q) for q in range(2)]
+        w1t = const.tile([P, GROUPS, 4 * F], U8, name="w1t", align_bytes=64)
+        w1t_i = w1t[:].rearrange("p g n -> p (g n)").bitcast(I32).rearrange("p (g n) -> p g n", g=GROUPS)
+        w1_i = w1_words.bitcast(I32).rearrange("g p n -> p g n")
+        w1s_hbm = w1_scales.bitcast(I32).rearrange("g r n -> r g n")
+        w2_raw = const.tile([P, 2 * F], U8, name="w2_raw", align_bytes=64)
+
+        nc.scalar.dma_start(out=pos4[0:B, :], in_=pos.rearrange("b n c -> b (n c)"))
+        nc.scalar.dma_start(out=pos32[0:BLOCKS, :], in_=pos.rearrange("b (k i) c -> (b k) (i c)", i=IB))
+        for q in range(2):
+            nc.sync.dma_start(out=h_sb[0][:, q * 1024 : q * 1024 + 1024], in_=h_flat[0:HALF, q * 1024 : q * 1024 + 1024])
+        for q in range(4):
+            nc.sync.dma_start(out=w1s_i[32 * q : 32 * q + 4], in_=w1s_hbm[4 * q : 4 * q + 4])
+        for n in (1, 0):
+            nc.sync.dma_start(out=w1t_i[:, :, n * 256 : n * 256 + 256], in_=w1_i[:, :, n * 256 : n * 256 + 256])
+        nc.scalar.dma_start(out=wr_raw[:], in_=wr.rearrange("(p t) -> p t", t=4))
+        nc.scalar.dma_start(out=gain_raw[:], in_=edge_gain.rearrange("(p t) -> p t", t=4))
+        nc.scalar.dma_start(out=gate_row[0:1, :], in_=gate_w.unsqueeze(0))
+        nc.sync.dma_start(out=w2_raw[:].bitcast(I32), in_=w2_words[0].bitcast(I32))
+        for q in range(4):
+            nc.sync.dma_start(
+                out=w2s_raw[32 * q : 32 * q + 4, :].bitcast(I32), in_=w2_scales[0, 4 * q : 4 * q + 4, :].bitcast(I32)
+            )
+        nc.sync.dma_start(out=h_sb[1][:], in_=h_flat[HALF:TOK, :])
+
+        sel_b = const.tile([P, P], BF16, name="sel_b")
+        sel_i = const.tile([P, P], BF16, name="sel_i")
+        sel_r = const.tile([P, BLOCKS], BF16, name="sel_r")
+        nc.vector.tensor_copy(
+            out=sel_b[:].rearrange("k (g b r) -> k g b r", g=4, b=4),
+            in_=ident[:, 0:4].unsqueeze(1).unsqueeze(3).to_broadcast([P, 4, 4, 8]),
+        )
+        nc.vector.tensor_copy(
+            out=sel_i[:].rearrange("k (g c) -> k g c", g=4), in_=ident[:, 0:32].unsqueeze(1).to_broadcast([P, 4, 32])
+        )
+        sel_f = const.tile([P, BLOCKS], F32, name="sel_f")
+        nc.vector.tensor_reduce(
+            out=sel_f[:], in_=ident[:, 0:96].rearrange("k (g c) -> k c g", g=3), axis=mybir.AxisListType.X, op=ALU.add
+        )
+        nc.vector.tensor_copy(out=sel_r[:], in_=sel_f[:])
+        pji = bank("pji")
+        nc.tensor.matmul(pji[:, 0 : N * 3], sel_b[:], pos4[:], start=True, stop=True)
+        nc.tensor.matmul(pji[:, N * 3 : N * 3 + IB * 3], sel_i[:], pos32[:], start=True, stop=True)
+        pi = const.tile([P, IB * 3], F32, name="pi")
+        diff = const.tile([P, 3, IB, N], F32, name="diff")
+        sq = const.tile([P, 3, ROWS], F32, name="sq")
+        r2 = const.tile([P, ROWS], F32, name="r2")
+        rem = const.tile([P, ROWS], F32, name="rem")
+        rem2 = const.tile([P, ROWS], F32, name="rem2")
+        mid = const.tile([P, ROWS], BF16, name="mid")
+        r2s = const.tile([P, ROWS], BF16, name="r2s")
+        nc.vector.tensor_copy(out=pi[:], in_=pji[:, N * 3 : N * 3 + IB * 3])
+        nc.vector.tensor_tensor(
+            out=diff[:],
+            in0=pji[:, 0 : N * 3].rearrange("p (j c) -> p c j", c=3).unsqueeze(2).to_broadcast([P, 3, IB, N]),
+            in1=pi[:].rearrange("p (i c) -> p c i", c=3).unsqueeze(3).to_broadcast([P, 3, IB, N]),
+            op=ALU.subtract,
+        )
+        nc.scalar.activation(
+            out=sq[:].rearrange("p c r -> p (c r)"), in_=diff[:].rearrange("p c i j -> p (c i j)"), func=ACT.Square
+        )
+
+        u_t = const.tile([P, 4, TOK], F32, name="u_t")
+        v_t = const.tile([P, 4, TOK], F32, name="v_t")
+        hg = [const.tile([P, GROUPS, HALF, 4], BF16, name="hg%d" % q, align_bytes=64) for q in range(2)]
+        hq = [const.tile([P, GROUPS * HALF], U32, name="hq%d" % q, align_bytes=64) for q in range(2)]
+        hs = [const.tile([P, GROUPS * HALF], U8, name="hs%d" % q, align_bytes=64) for q in range(2)]
+
+        def turn_h(q, pair, copy):
+            words = h_sb[q][:].bitcast(F32)
+            xt = bank("xt")
+            xv = xt[:].rearrange("p (g u r) -> p g u r", g=2, u=2)
+            for gg in range(2):
+                g = 2 * pair + gg
+                for u in range(2):
+                    nc.tensor.transpose(xv[:, gg, u, :], words[:, 256 * g + u : 256 * (g + 1) : 2], ident[:])
+            dst = hg[q][:].rearrange("p g r t -> p (g r t)").bitcast(F32).rearrange("p (g r u) -> p g r u", g=GROUPS, u=2)
+            copy(out=dst[:, 2 * pair : 2 * pair + 2], in_=xv.rearrange("p g u r -> p g r u"))
+
+        def quant_h(q):
+            nc.vector.quantize_mx(
+                out=hq[q][:].bitcast(FP8X4), scales=hs[q][:], in_=hg[q][:].rearrange("p g r t -> p (g r t)")
+            )
+
+        uv_sb = {}
+
+        def project(q, n, copy):
+            acc = bank("acc")
+            for g in range(GROUPS):
+                cols = slice(g * HALF, (g + 1) * HALF)
+                nc.tensor.matmul_mx(
+                    out=acc[:],
+                    lhsT=hq[q][:, cols].bitcast(FP8X4),
+                    lhsT_scale=hs[q][:, cols],
+                    rhs=w1t[:, g, n * 1024 : n * 1024 + 1024].bitcast(FP4X4),
+                    rhs_scale=w1s[:, g, n * 512 : n * 512 + 512],
+                    start=(g == 0),
+                    stop=(g == GROUPS - 1),
+                )
+            uv = const.tile([P, 4, P], F32, name="uv%d%d" % (q, n))
+            uv_sb[q, n] = uv
+            copy(out=uv[:], in_=acc[:].rearrange("q (p t) -> q t p", t=4))
+
+        def turn_uv(q, n, copy):
+            uvt = bank("uvt")
+            for t in range(4):
+                nc.tensor.transpose(uvt[:, t * P : t * P + P], uv_sb[q, n][:, t, :], ident[:])
+            dst = v_t if n else u_t
+            copy(out=dst[:, :, q * HALF : (q + 1) * HALF], in_=uvt[:].rearrange("p (t r) -> p t r", t=4))
+
+        turn_h(0, 0, nc.scalar.copy)
+        turn_h(0, 1, nc.vector.tensor_copy)
+        quant_h(0)
+        nc.vector.tensor_tensor(out=r2[:], in0=sq[:, 0, :], in1=sq[:, 1, :], op=ALU.add)
+        nc.vector.tensor_tensor(out=r2[:], in0=r2[:], in1=sq[:, 2, :], op=ALU.add)
+        nc.vector.tensor_copy(out=r2s[:], in_=r2[:])
+        nc.vector.tensor_tensor(out=rem[:], in0=r2[:], in1=r2s[:], op=ALU.subtract)
+        nc.vector.tensor_copy(out=mid[:], in_=rem[:])
+        nc.vector.tensor_tensor(out=rem2[64:128, :], in0=rem[64:128, :], in1=mid[64:128, :], op=ALU.subtract)
+        nc.vector.tensor_copy(out=r2s[32:64, :], in_=mid[32:64, :])
+        nc.vector.tensor_copy(out=r2s[64:128, :], in_=rem2[64:128, :])
+        nc.vector.tensor_copy(out=wg[:, 0, :], in_=wr_raw[:])
+        nc.vector.tensor_copy(out=wg[:, 1, :], in_=gain_raw[:])
+        project(0, 1, nc.scalar.copy)
+        turn_uv(0, 1, nc.vector.tensor_copy)
+        project(0, 0, nc.scalar.copy)
+        turn_uv(0, 0, nc.scalar.copy)
+
+        nc.gpsimd.tensor_copy(
+            out=gate_perm[:].rearrange("k (t p) -> k t p", t=4), in_=gate_row[:].rearrange("k (p t) -> k t p", t=4)
+        )
+        gw = psum.tile([P, F], F32, name="gw", tag="gw", bufs=1)
+        nc.tensor.matmul(gw[:], ones[:], gate_perm[:], start=True, stop=True)
+        w2p = const.tile([P, 2 * F], U8, name="w2p", align_bytes=64)
+        w2sp = const.tile([P, F], U8, name="w2sp", align_bytes=64)
+        nc.gpsimd.tensor_copy(
+            out=w2p[:].rearrange("k (t p w) -> k p t w", t=4, w=2), in_=w2_raw[:].rearrange("k (p t w) -> k p t w", t=4, w=2)
+        )
+        nc.gpsimd.tensor_copy(
+            out=w2sp[:].rearrange("k (t p) -> k p t", t=4), in_=w2s_raw[:].rearrange("k (p t) -> k p t", t=4)
+        )
+
+        r2p, pre, act, abf, aq, asc, yb, mt, gp, gm = {}, {}, {}, {}, {}, {}, {}, {}, {}, {}
+        outp = {}
+
+        def spread_r2(k):
+            r2p[k] = psum.tile([P, ROWS], F32, name="r2p", tag="r2p", bufs=2)
+            nc.tensor.matmul(
+                r2p[k][:], sel_r[:, k : k + 1].to_broadcast([P, P]), r2s[:], start=True, stop=True
+            )
+
+        def edge_sum(k, t):
+            b = k // (N // IB)
+            if t == 0:
+                pre[k] = work.tile([P, 4, ROWS], F32, name="pre")
+            nc.vector.scalar_tensor_tensor(
+                out=pre[k][:, t, :].rearrange("p (i j) -> p i j", i=IB),
+                in0=r2p[k][:].rearrange("p (i j) -> p i j", i=IB),
+                scalar=wg[:, 0, t : t + 1],
+                in1=v_t[:, t, b * N : (b + 1) * N].unsqueeze(1).to_broadcast([P, IB, N]),
+                op0=ALU.mult,
+                op1=ALU.add,
+            )
+
+        def edge_silu(k, t):
+            if t == 0:
+                act[k] = work.tile([P, 4, ROWS], F32, name="act")
+            for i in range(IB):
+                tok = k * IB + i
+                nc.scalar.activation(
+                    out=act[k][:, t, i * N : i * N + N],
+                    in_=pre[k][:, t, i * N : i * N + N],
+                    func=ACT.Silu,
+                    bias=u_t[:, t, tok : tok + 1],
+                )
+
+        def edge_gain_mul(k, q):
+            if q == 0:
+                abf[k] = work.tile([P, ROWS, 4], BF16, name="abf", align_bytes=64)
+            rows = slice(q * P, q * P + P)
+            nc.gpsimd.tensor_tensor(
+                out=abf[k][:, rows, :],
+                in0=act[k][:, :, rows].rearrange("p t r -> p r t"),
+                in1=wg[:, 1, :].unsqueeze(1).to_broadcast([P, P, 4]),
+                op=ALU.mult,
+            )
+
+        def edge_quant(k):
+            aq[k] = work.tile([P, ROWS], U32, name="aq", align_bytes=64)
+            asc[k] = work.tile([P, ROWS], U8, name="asc", align_bytes=64)
+            nc.vector.quantize_mx(
+                out=aq[k][:].bitcast(FP8X4), scales=asc[k][:], in_=abf[k][:].rearrange("p r t -> p (r t)")
+            )
+
+        def msg_matmul(j):
+            k, rt = divmod(j, TILES)
+            cols = slice(rt * P, rt * P + P)
+            yb[j] = bank("y")
+            nc.tensor.matmul_mx(
+                out=yb[j][:],
+                lhsT=aq[k][:, cols].bitcast(FP8X4),
+                lhsT_scale=asc[k][:, cols],
+                rhs=w2p[:].bitcast(FP4X4),
+                rhs_scale=w2sp[:],
+                start=True,
+                stop=True,
+            )
+
+        def msg_silu(j):
+            mt[j] = msgs.tile([P, F], F32, name="mt")
+            nc.scalar.activation(out=mt[j][:], in_=yb[j][:], func=ACT.Silu)
+
+        def msg_gate(j):
+            k, rt = divmod(j, TILES)
+            if rt == 0:
+                gp[k] = work.tile([P, TILES], F32, name="gp")
+            prod = work.tile([P, F], F32, name="prod")
+            nc.vector.scalar_tensor_tensor(
+                out=prod[:],
+                in0=mt[j][:],
+                scalar=1.0,
+                in1=gw[:],
+                op0=ALU.mult,
+                op1=ALU.mult,
+                accum_out=gp[k][:, rt : rt + 1],
+            )
+
+        def gate(k):
+            th = work.tile([P, TILES], F32, name="th")
+            gm[k] = work.tile([P, TILES, 2], F32, name="gm")
+            nc.scalar.activation(out=th[:], in_=gp[k][:], func=ACT.Tanh, scale=0.5)
+            for s in range(2):
+                nc.scalar.activation(
+                    out=gm[k][:, :, s],
+                    in_=th[:],
+                    func=ACT.Identity,
+                    scale=mask[:, s : s + 1],
+                    bias=mask[:, s : s + 1],
+                )
+
+        def gather(j):
+            k, rt = divmod(j, TILES)
+            q, col = divmod(2 * j, HALF)
+            if col == 0:
+                outp[q] = psum.tile([P, 4, HALF], F32, name="outp", tag="outp", bufs=1)
+            for t in range(4):
+                nc.tensor.matmul(
+                    outp[q][:, t, col : col + 2],
+                    mt[j][:, t * P : t * P + P],
+                    gm[k][:, rt, :],
+                    start=True,
+                    stop=True,
+                )
+
+        def finish(q):
+            o_sb = const.tile([P, 4, HALF], F32, name="o_sb%d" % q)
+            o_bf = const.tile([P, HALF, 4], BF16, name="o_bf%d" % q, align_bytes=64)
+            o_q = const.tile([P, HALF], U32, name="o_q%d" % q, align_bytes=64)
+            o_s = const.tile([P, HALF], U8, name="o_s%d" % q, align_bytes=64)
+            o_t = const.tile([P, P, 4], F32, name="o_t%d" % q)
+            nc.vector.tensor_copy(out=o_sb[:], in_=outp[q][:])
+            nc.scalar.copy(out=o_bf[:], in_=outp[q][:].rearrange("p t r -> p r t"))
+            ob = bank("ob")
+            for t in range(4):
+                nc.tensor.transpose(ob[:, t * P : t * P + P], o_sb[:, t, :], ident[:])
+            nc.vector.quantize_mx(out=o_q[:].bitcast(FP8X4), scales=o_s[:], in_=o_bf[:].rearrange("p r t -> p (r t)"))
+            nc.scalar.copy(out=o_t[:], in_=ob[:].rearrange("q (t p) -> q p t", t=4))
+            toks = slice(q * HALF, (q + 1) * HALF)
+            nc.sync.dma_start(
+                out=out_1[0].rearrange("p m t -> p (m t)")[:, q * 512 : q * 512 + 512].bitcast(I32), in_=o_q[:].bitcast(I32)
+            )
+            for s in range(4):
+                nc.sync.dma_start(
+                    out=out_2[0, 4 * s : 4 * s + 4, toks].bitcast(I32), in_=o_s[32 * s : 32 * s + 4, :].bitcast(I32)
+                )
+            nc.sync.dma_start(
+                out=out_0.rearrange("b n f -> (b n) f")[toks, :], in_=o_t[:].rearrange("q p t -> q (p t)")
+            )
+
+        n_tiles = BLOCKS * TILES
+        late = {
+            2: lambda: turn_h(1, 0, nc.vector.tensor_copy),
+            4: lambda: turn_h(1, 1, nc.vector.tensor_copy),
+            6: lambda: quant_h(1),
+            7: lambda: project(1, 1, nc.vector.tensor_copy),
+            9: lambda: turn_uv(1, 1, nc.vector.tensor_copy),
+            10: lambda: project(1, 0, nc.vector.tensor_copy),
+            12: lambda: turn_uv(1, 0, nc.vector.tensor_copy),
+        }
+
+        def go(idx, count, fn):
+            if 0 <= idx < count:
+                fn(idx)
+
+        spread_r2(0)
+        for n in range(n_tiles + 24):
+            k, q = divmod(n, 4)
+            if q == 0:
+                go(k + 1, BLOCKS, spread_r2)
+            go(n - 14, n_tiles, msg_matmul)
+            go(n - 23, n_tiles, gather)
+            if k < BLOCKS:
+                edge_sum(k, q)
+            if q == 1:
+                go(k - 3, BLOCKS, edge_quant)
+            if 0 <= k - 1 < BLOCKS:
+                edge_silu(k - 1, q)
+            if q == 1:
+                go(k - 5, BLOCKS, gate)
+            go(n - 15, n_tiles, msg_silu)
+            if 0 <= k - 2 < BLOCKS:
+                edge_gain_mul(k - 2, q)
+            go(n - 17, n_tiles, msg_gate)
+            if n in late:
+                late[n]()
+            if n - 23 == n_tiles // 2 - 1:
+                finish(0)
+        finish(1)

@@ -32,18 +32,20 @@ def tile_egnngatededgelayer_x2_kernel(
     with ExitStack() as ctx:
         const = ctx.enter_context(tc.tile_pool(name="const", bufs=1))
         work = ctx.enter_context(tc.tile_pool(name="work", bufs=3))
-        msgs = ctx.enter_context(tc.tile_pool(name="msgs", bufs=12))
+        msgs = ctx.enter_context(tc.tile_pool(name="msgs", bufs=18))
         psum = ctx.enter_context(tc.psum_pool(name="psum", bufs=1))
         ctx.enter_context(tc.manual_schedule())
 
         def bank(name):
-            return psum.tile([P, 512], F32, name=name, tag="mm", bufs=4)
+            return psum.tile([P, 512], F32, name=name, tag="mm", bufs=3)
 
         w1s = const.tile([P, GROUPS, 2 * F], U8, name="w1s", align_bytes=64)
         w1s_i = w1s[:].rearrange("p g n -> p (g n)").bitcast(I32).rearrange("p (g n) -> p g n", g=GROUPS)
         w2s_raw = const.tile([P, F], U8, name="w2s_raw", align_bytes=64)
-        pos4 = const.tile([P, N * 3], BF16, name="pos4")
-        pos32 = const.tile([P, IB * 3], BF16, name="pos32")
+        pos_row = const.tile([P, TOK * 3], BF16, name="pos_row")
+        pos_j = const.tile([P, B, 3], BF16, name="pos_j")
+        gms = [const.tile([P, TILES, 2 * P], F32, name="gm%d" % q) for q in range(4)]
+        zero = const.tile([P, P], F32, name="zero")
         gate_row = const.tile([P, F], BF16, name="gate_row")
         gate_perm = const.tile([P, F], BF16, name="gate_perm")
         ones = const.tile([P, P], BF16, name="ones")
@@ -53,13 +55,15 @@ def tile_egnngatededgelayer_x2_kernel(
         gain_raw = const.tile([P, 4], BF16, name="gain_raw")
         wg = const.tile([P, 2, 4], F32, name="wg")
 
-        nc.vector.memset(pos4[:], 0.0)
-        nc.vector.memset(pos32[:], 0.0)
+        nc.vector.memset(pos_row[:], 0.0)
+        nc.gpsimd.memset(ones[:], 1.0)
         make_identity(nc, ident[:])
         nc.vector.memset(w1s[:].rearrange("p g n -> p (g n)").bitcast(I32), 0)
         nc.gpsimd.memset(gate_row[:], 0.0)
         nc.gpsimd.memset(w2s_raw[:].bitcast(I32), 0)
-        nc.gpsimd.memset(ones[:], 1.0)
+        nc.gpsimd.memset(zero[:], 0.0)
+        for q in range(4):
+            nc.gpsimd.memset(gms[q][:], 0.0)
         for s in range(2):
             for v in range(2):
                 nc.gpsimd.memset(mask[64 * v : 64 * v + 64, s : s + 1], 0.0625 if s == v else 0.0)
@@ -72,8 +76,9 @@ def tile_egnngatededgelayer_x2_kernel(
         w1s_hbm = w1_scales.bitcast(I32).rearrange("g r n -> r g n")
         w2_raw = const.tile([P, 2 * F], U8, name="w2_raw", align_bytes=64)
 
-        nc.scalar.dma_start(out=pos4[0:B, :], in_=pos.rearrange("b n c -> b (n c)"))
-        nc.scalar.dma_start(out=pos32[0:BLOCKS, :], in_=pos.rearrange("b (k i) c -> (b k) (i c)", i=IB))
+        nc.scalar.dma_start(out=pos_row[0:1, :], in_=pos.rearrange("b n c -> (b n c)").unsqueeze(0))
+        for v in range(2):
+            nc.scalar.dma_start(out=pos_j[64 * v : 64 * v + 64], in_=pos.rearrange("b j c -> j b c"))
         for q in range(2):
             nc.sync.dma_start(out=h_sb[0][:, q * 1024 : q * 1024 + 1024], in_=h_flat[0:HALF, q * 1024 : q * 1024 + 1024])
         for q in range(4):
@@ -90,41 +95,24 @@ def tile_egnngatededgelayer_x2_kernel(
             )
         nc.sync.dma_start(out=h_sb[1][:], in_=h_flat[HALF:TOK, :])
 
-        sel_b = const.tile([P, P], BF16, name="sel_b")
-        sel_i = const.tile([P, P], BF16, name="sel_i")
-        sel_r = const.tile([P, BLOCKS], BF16, name="sel_r")
-        nc.vector.tensor_copy(
-            out=sel_b[:].rearrange("k (g b r) -> k g b r", g=4, b=4),
-            in_=ident[:, 0:4].unsqueeze(1).unsqueeze(3).to_broadcast([P, 4, 4, 8]),
-        )
-        nc.vector.tensor_copy(
-            out=sel_i[:].rearrange("k (g c) -> k g c", g=4), in_=ident[:, 0:32].unsqueeze(1).to_broadcast([P, 4, 32])
-        )
-        sel_f = const.tile([P, BLOCKS], F32, name="sel_f")
-        nc.vector.tensor_reduce(
-            out=sel_f[:], in_=ident[:, 0:96].rearrange("k (g c) -> k c g", g=3), axis=mybir.AxisListType.X, op=ALU.add
-        )
-        nc.vector.tensor_copy(out=sel_r[:], in_=sel_f[:])
-        pji = bank("pji")
-        nc.tensor.matmul(pji[:, 0 : N * 3], sel_b[:], pos4[:], start=True, stop=True)
-        nc.tensor.matmul(pji[:, N * 3 : N * 3 + IB * 3], sel_i[:], pos32[:], start=True, stop=True)
-        pi = const.tile([P, IB * 3], F32, name="pi")
-        diff = const.tile([P, 3, IB, N], F32, name="diff")
-        sq = const.tile([P, 3, ROWS], F32, name="sq")
-        r2 = const.tile([P, ROWS], F32, name="r2")
-        rem = const.tile([P, ROWS], F32, name="rem")
-        rem2 = const.tile([P, ROWS], F32, name="rem2")
-        mid = const.tile([P, ROWS], BF16, name="mid")
-        r2s = const.tile([P, ROWS], BF16, name="r2s")
-        nc.vector.tensor_copy(out=pi[:], in_=pji[:, N * 3 : N * 3 + IB * 3])
-        nc.vector.tensor_tensor(
-            out=diff[:],
-            in0=pji[:, 0 : N * 3].rearrange("p (j c) -> p c j", c=3).unsqueeze(2).to_broadcast([P, 3, IB, N]),
-            in1=pi[:].rearrange("p (i c) -> p c i", c=3).unsqueeze(3).to_broadcast([P, 3, IB, N]),
-            op=ALU.subtract,
-        )
+        sqd = const.tile([P, TOK // 2, 3], F32, name="sqd")
+        r2c = const.tile([P, TOK // 2], F32, name="r2c")
+        for half in range(2):
+            pb = bank("pb")
+            nc.tensor.matmul(
+                pb[:, 0:384], ones[:], pos_row[:, half * 384 : half * 384 + 384], start=True, stop=True
+            )
+            pv = pb[:, 0:384].rearrange("p (b i v c) -> p b i v c", b=2, v=2, c=3)
+            for v in range(2):
+                rows = slice(64 * v, 64 * v + 64)
+                nc.vector.tensor_tensor(
+                    out=sqd[rows, half * 64 : half * 64 + 64, :].rearrange("p (b i) c -> p b i c", b=2),
+                    in0=pv[rows, :, :, v, :],
+                    in1=pos_j[rows, 2 * half : 2 * half + 2, :].unsqueeze(2).to_broadcast([64, 2, 32, 3]),
+                    op=ALU.subtract,
+                )
         nc.scalar.activation(
-            out=sq[:].rearrange("p c r -> p (c r)"), in_=diff[:].rearrange("p c i j -> p (c i j)"), func=ACT.Square
+            out=sqd[:].rearrange("p r c -> p (r c)"), in_=sqd[:].rearrange("p r c -> p (r c)"), func=ACT.Square
         )
 
         u_t = const.tile([P, 4, TOK], F32, name="u_t")
@@ -175,20 +163,24 @@ def tile_egnngatededgelayer_x2_kernel(
             dst = v_t if n else u_t
             copy(out=dst[:, :, q * HALF : (q + 1) * HALF], in_=uvt[:].rearrange("p (t r) -> p t r", t=4))
 
+        r2p = {}
+
+        def spread_r2(k):
+            r2p[k] = psum.tile([P, ROWS], F32, name="r2p", tag="r2p", bufs=2)
+            for rt in range(TILES):
+                j = k * TILES + rt
+                nc.tensor.transpose(
+                    r2p[k][:, rt * P : rt * P + P], r2c[:, j : j + 1].to_broadcast([P, P]), ident[:]
+                )
+
         turn_h(0, 0, nc.scalar.copy)
         turn_h(0, 1, nc.vector.tensor_copy)
         quant_h(0)
-        nc.vector.tensor_tensor(out=r2[:], in0=sq[:, 0, :], in1=sq[:, 1, :], op=ALU.add)
-        nc.vector.tensor_tensor(out=r2[:], in0=r2[:], in1=sq[:, 2, :], op=ALU.add)
-        nc.vector.tensor_copy(out=r2s[:], in_=r2[:])
-        nc.vector.tensor_tensor(out=rem[:], in0=r2[:], in1=r2s[:], op=ALU.subtract)
-        nc.vector.tensor_copy(out=mid[:], in_=rem[:])
-        nc.vector.tensor_tensor(out=rem2[64:128, :], in0=rem[64:128, :], in1=mid[64:128, :], op=ALU.subtract)
-        nc.vector.tensor_copy(out=r2s[32:64, :], in_=mid[32:64, :])
-        nc.vector.tensor_copy(out=r2s[64:128, :], in_=rem2[64:128, :])
+        nc.vector.tensor_reduce(out=r2c[:], in_=sqd[:], axis=mybir.AxisListType.X, op=ALU.add)
         nc.vector.tensor_copy(out=wg[:, 0, :], in_=wr_raw[:])
         nc.vector.tensor_copy(out=wg[:, 1, :], in_=gain_raw[:])
         project(0, 1, nc.scalar.copy)
+        spread_r2(0)
         turn_uv(0, 1, nc.vector.tensor_copy)
         project(0, 0, nc.scalar.copy)
         turn_uv(0, 0, nc.scalar.copy)
@@ -207,14 +199,8 @@ def tile_egnngatededgelayer_x2_kernel(
             out=w2sp[:].rearrange("k (t p) -> k p t", t=4), in_=w2s_raw[:].rearrange("k (p t) -> k p t", t=4)
         )
 
-        r2p, pre, act, abf, aq, asc, yb, mt, gp, gm = {}, {}, {}, {}, {}, {}, {}, {}, {}, {}
+        pre, act, abf, aq, asc, yb, mt, gp, gm = {}, {}, {}, {}, {}, {}, {}, {}, {}
         outp = {}
-
-        def spread_r2(k):
-            r2p[k] = psum.tile([P, ROWS], F32, name="r2p", tag="r2p", bufs=2)
-            nc.tensor.matmul(
-                r2p[k][:], sel_r[:, k : k + 1].to_broadcast([P, P]), r2s[:], start=True, stop=True
-            )
 
         def edge_sum(k, t):
             b = k // (N // IB)
@@ -231,7 +217,7 @@ def tile_egnngatededgelayer_x2_kernel(
 
         def edge_silu(k, t):
             if t == 0:
-                act[k] = work.tile([P, 4, ROWS], F32, name="act")
+                act[k] = work.tile([P, 4, ROWS], F32, name="act", bufs=4)
             for i in range(IB):
                 tok = k * IB + i
                 nc.scalar.activation(
@@ -243,18 +229,19 @@ def tile_egnngatededgelayer_x2_kernel(
 
         def edge_gain_mul(k, q):
             if q == 0:
-                abf[k] = work.tile([P, ROWS, 4], BF16, name="abf", align_bytes=64)
-            rows = slice(q * P, q * P + P)
-            nc.gpsimd.tensor_tensor(
-                out=abf[k][:, rows, :],
-                in0=act[k][:, :, rows].rearrange("p t r -> p r t"),
-                in1=wg[:, 1, :].unsqueeze(1).to_broadcast([P, P, 4]),
+                abf[k] = work.tile([P, ROWS, 4], BF16, name="abf", align_bytes=64, bufs=4)
+            eng = nc.vector if k >= BLOCKS - 2 and q % 2 else nc.gpsimd
+            r0 = q * P
+            eng.tensor_tensor(
+                out=abf[k][:, r0 : r0 + P, :].rearrange("p (c i) t -> p c t i", i=4),
+                in0=act[k][:, :, r0 : r0 + P].rearrange("p t (c i) -> p c t i", i=4),
+                in1=wg[:, 1, :].unsqueeze(1).unsqueeze(3).to_broadcast([P, P // 4, 4, 4]),
                 op=ALU.mult,
             )
 
         def edge_quant(k):
-            aq[k] = work.tile([P, ROWS], U32, name="aq", align_bytes=64)
-            asc[k] = work.tile([P, ROWS], U8, name="asc", align_bytes=64)
+            aq[k] = work.tile([P, ROWS], U32, name="aq", align_bytes=64, bufs=4)
+            asc[k] = work.tile([P, ROWS], U8, name="asc", align_bytes=64, bufs=4)
             nc.vector.quantize_mx(
                 out=aq[k][:].bitcast(FP8X4), scales=asc[k][:], in_=abf[k][:].rearrange("p r t -> p (r t)")
             )
@@ -292,46 +279,85 @@ def tile_egnngatededgelayer_x2_kernel(
                 accum_out=gp[k][:, rt : rt + 1],
             )
 
-        def gate(k):
+        def gate(k, lo=0, hi=TILES):
             th = work.tile([P, TILES], F32, name="th")
-            gm[k] = work.tile([P, TILES, 2], F32, name="gm")
-            nc.scalar.activation(out=th[:], in_=gp[k][:], func=ACT.Tanh, scale=0.5)
+            gm[k] = gms[k % 4]
+            nc.scalar.activation(out=th[:, lo:hi], in_=gp[k][:, lo:hi], func=ACT.Tanh, scale=0.5)
             for s in range(2):
                 nc.scalar.activation(
-                    out=gm[k][:, :, s],
-                    in_=th[:],
+                    out=gm[k][:, lo:hi, 126 + s],
+                    in_=th[:, lo:hi],
                     func=ACT.Identity,
                     scale=mask[:, s : s + 1],
                     bias=mask[:, s : s + 1],
                 )
+
+        def wide(j):
+            return j % 5 in (1, 3) and j % 64 < 60
+
+        outm = {}
 
         def gather(j):
             k, rt = divmod(j, TILES)
             q, col = divmod(2 * j, HALF)
             if col == 0:
                 outp[q] = psum.tile([P, 4, HALF], F32, name="outp", tag="outp", bufs=1)
-            for t in range(4):
+                outm[q] = psum.tile([P, F], F32, name="outm", tag="outm", bufs=1)
+                for t in range(4):
+                    nc.tensor.transpose(outp[q][:, t, :], zero[:], ident[:])
+            wides = [x for x in range(q * 64, q * 64 + 64) if wide(x)]
+            if wide(j):
                 nc.tensor.matmul(
-                    outp[q][:, t, col : col + 2],
-                    mt[j][:, t * P : t * P + P],
-                    gm[k][:, rt, :],
-                    start=True,
-                    stop=True,
+                    outm[q][:],
+                    gm[k][:, rt, 126 - col : 254 - col],
+                    mt[j][:],
+                    start=(j == wides[0]),
+                    stop=(j == wides[-1]),
                 )
+            else:
+                for t in range(4):
+                    nc.tensor.matmul(
+                        outp[q][:, t, col : col + 2],
+                        mt[j][:, t * P : t * P + P],
+                        gm[k][:, rt, 126:128],
+                        start=True,
+                        stop=True,
+                    )
+
+        sums = {}
+
+        def take_sums(q):
+            o_m = const.tile([P, F], F32, name="o_m%d" % q)
+            o_p = const.tile([P, 4, HALF], F32, name="o_p%d" % q)
+            nc.vector.tensor_copy(out=o_m[:], in_=outm[q][:])
+            nc.scalar.copy(out=o_p[:], in_=outp[q][:])
+            sums[q] = (o_m, o_p)
 
         def finish(q):
-            o_sb = const.tile([P, 4, HALF], F32, name="o_sb%d" % q)
+            o_m, o_p = sums[q]
             o_bf = const.tile([P, HALF, 4], BF16, name="o_bf%d" % q, align_bytes=64)
             o_q = const.tile([P, HALF], U32, name="o_q%d" % q, align_bytes=64)
             o_s = const.tile([P, HALF], U8, name="o_s%d" % q, align_bytes=64)
             o_t = const.tile([P, P, 4], F32, name="o_t%d" % q)
-            nc.vector.tensor_copy(out=o_sb[:], in_=outp[q][:])
-            nc.scalar.copy(out=o_bf[:], in_=outp[q][:].rearrange("p t r -> p r t"))
+            pl = bank("pl")
+            for t in range(4):
+                nc.tensor.transpose(pl[:, t * P : t * P + P], o_m[:, t * P : t * P + P], ident[:])
             ob = bank("ob")
             for t in range(4):
-                nc.tensor.transpose(ob[:, t * P : t * P + P], o_sb[:, t, :], ident[:])
+                nc.tensor.transpose(ob[:, t * P : t * P + P], o_p[:, t, :], ident[:])
+            nc.vector.tensor_tensor(
+                out=o_bf[:],
+                in0=pl[:].rearrange("p (t r) -> p r t", t=4),
+                in1=o_p[:].rearrange("p t r -> p r t"),
+                op=ALU.add,
+            )
+            nc.vector.tensor_tensor(
+                out=o_t[:],
+                in0=ob[:].rearrange("q (t p) -> q p t", t=4),
+                in1=o_m[:].rearrange("q (t p) -> q p t", t=4),
+                op=ALU.add,
+            )
             nc.vector.quantize_mx(out=o_q[:].bitcast(FP8X4), scales=o_s[:], in_=o_bf[:].rearrange("p r t -> p (r t)"))
-            nc.scalar.copy(out=o_t[:], in_=ob[:].rearrange("q (t p) -> q p t", t=4))
             toks = slice(q * HALF, (q + 1) * HALF)
             nc.sync.dma_start(
                 out=out_1[0].rearrange("p m t -> p (m t)")[:, q * 512 : q * 512 + 512].bitcast(I32), in_=o_q[:].bitcast(I32)
@@ -359,27 +385,34 @@ def tile_egnngatededgelayer_x2_kernel(
             if 0 <= idx < count:
                 fn(idx)
 
-        spread_r2(0)
-        for n in range(n_tiles + 24):
+        for n in range(n_tiles + 26):
             k, q = divmod(n, 4)
-            if q == 0:
+            half = n_tiles // 2
+            go(n - 15, n_tiles, msg_matmul)
+            go(n - 21, half, gather)
+            if n - 25 >= half:
+                go(n - 25, n_tiles, gather)
+            if q == 1:
                 go(k + 1, BLOCKS, spread_r2)
-            go(n - 14, n_tiles, msg_matmul)
-            go(n - 23, n_tiles, gather)
             if k < BLOCKS:
                 edge_sum(k, q)
+            if 0 <= n - 3 < n_tiles:
+                edge_silu((n - 3) // 4, (n - 3) % 4)
+            if 0 <= n - 8 < n_tiles:
+                edge_gain_mul((n - 8) // 4, (n - 8) % 4)
+            if q == 0:
+                go(k - 5, BLOCKS - 1, gate)
+            if n - 18 == n_tiles - 1 or n - 20 == n_tiles - 1:
+                gate(BLOCKS - 1, 0 if n - 18 == n_tiles - 1 else 2, 2 if n - 18 == n_tiles - 1 else 4)
+            go(n - 15, n_tiles, msg_silu)
             if q == 1:
                 go(k - 3, BLOCKS, edge_quant)
-            if 0 <= k - 1 < BLOCKS:
-                edge_silu(k - 1, q)
-            if q == 1:
-                go(k - 5, BLOCKS, gate)
-            go(n - 15, n_tiles, msg_silu)
-            if 0 <= k - 2 < BLOCKS:
-                edge_gain_mul(k - 2, q)
-            go(n - 17, n_tiles, msg_gate)
+            go(n - 15, n_tiles, msg_gate)
             if n in late:
                 late[n]()
-            if n - 23 == n_tiles // 2 - 1:
+            if n - 23 == half - 1:
+                take_sums(0)
+            if n - 29 == half - 1:
                 finish(0)
+        take_sums(1)
         finish(1)

@@ -42,8 +42,8 @@ def tile_egnngatededgelayer_x2_kernel(
         w1s = const.tile([P, GROUPS, 2 * F], U8, name="w1s", align_bytes=64)
         w1s_i = w1s[:].rearrange("p g n -> p (g n)").bitcast(I32).rearrange("p (g n) -> p g n", g=GROUPS)
         w2s_raw = const.tile([P, F], U8, name="w2s_raw", align_bytes=64)
-        pos_row = const.tile([P, TOK * 3], BF16, name="pos_row")
-        pos_j = const.tile([P, B, 3], BF16, name="pos_j")
+        pos_i = const.tile([P, 2, 3], BF16, name="pos_i")
+        pos_j = const.tile([P, N, 3], BF16, name="pos_j")
         gms = [const.tile([P, TILES, 2 * P], F32, name="gm%d" % q) for q in range(4)]
         zero = const.tile([P, P], F32, name="zero")
         gate_row = const.tile([P, F], BF16, name="gate_row")
@@ -55,10 +55,9 @@ def tile_egnngatededgelayer_x2_kernel(
         gain_raw = const.tile([P, 4], BF16, name="gain_raw")
         wg = const.tile([P, 2, 4], F32, name="wg")
 
-        nc.vector.memset(pos_row[:], 0.0)
-        nc.gpsimd.memset(ones[:], 1.0)
-        make_identity(nc, ident[:])
         nc.vector.memset(w1s[:].rearrange("p g n -> p (g n)").bitcast(I32), 0)
+        make_identity(nc, ident[:])
+        nc.gpsimd.memset(ones[:], 1.0)
         nc.gpsimd.memset(gate_row[:], 0.0)
         nc.gpsimd.memset(w2s_raw[:].bitcast(I32), 0)
         nc.gpsimd.memset(zero[:], 0.0)
@@ -76,9 +75,12 @@ def tile_egnngatededgelayer_x2_kernel(
         w1s_hbm = w1_scales.bitcast(I32).rearrange("g r n -> r g n")
         w2_raw = const.tile([P, 2 * F], U8, name="w2_raw", align_bytes=64)
 
-        nc.scalar.dma_start(out=pos_row[0:1, :], in_=pos.rearrange("b n c -> (b n c)").unsqueeze(0))
-        for v in range(2):
-            nc.scalar.dma_start(out=pos_j[64 * v : 64 * v + 64], in_=pos.rearrange("b j c -> j b c"))
+        nc.scalar.dma_start(out=pos_i[:], in_=pos.rearrange("b (i v) c -> (b i) v c", v=2))
+        for b in range(B):
+            nc.scalar.dma_start(
+                out=pos_j[32 * b : 32 * b + 32].rearrange("p j c -> p (j c)"),
+                in_=pos[b].rearrange("j c -> (j c)").partition_broadcast(32),
+            )
         for q in range(2):
             nc.sync.dma_start(out=h_sb[0][:, q * 1024 : q * 1024 + 1024], in_=h_flat[0:HALF, q * 1024 : q * 1024 + 1024])
         for q in range(4):
@@ -95,28 +97,26 @@ def tile_egnngatededgelayer_x2_kernel(
             )
         nc.sync.dma_start(out=h_sb[1][:], in_=h_flat[HALF:TOK, :])
 
-        sqd = const.tile([P, TOK // 2, 3], F32, name="sqd")
-        r2c = const.tile([P, TOK // 2], F32, name="r2c")
-        for half in range(2):
-            pb = bank("pb")
-            nc.tensor.matmul(
-                pb[:, 0:384], ones[:], pos_row[:, half * 384 : half * 384 + 384], start=True, stop=True
-            )
-            pv = pb[:, 0:384].rearrange("p (b i v c) -> p b i v c", b=2, v=2, c=3)
-            for v in range(2):
-                rows = slice(64 * v, 64 * v + 64)
-                nc.vector.tensor_tensor(
-                    out=sqd[rows, half * 64 : half * 64 + 64, :].rearrange("p (b i) c -> p b i c", b=2),
-                    in0=pv[rows, :, :, v, :],
-                    in1=pos_j[rows, 2 * half : 2 * half + 2, :].unsqueeze(2).to_broadcast([64, 2, 32, 3]),
-                    op=ALU.subtract,
-                )
+        sqd = const.tile([P, 2, N, 3], F32, name="sqd")
+        r2c = const.tile([P, 2, N], F32, name="r2c")
+        out_flat = out_0.rearrange("b n f -> (b n) f")
+        nc.vector.tensor_tensor(
+            out=sqd[:],
+            in0=pos_j[:].unsqueeze(1).to_broadcast([P, 2, N, 3]),
+            in1=pos_i[:].unsqueeze(2).to_broadcast([P, 2, N, 3]),
+            op=ALU.subtract,
+        )
         nc.scalar.activation(
-            out=sqd[:].rearrange("p r c -> p (r c)"), in_=sqd[:].rearrange("p r c -> p (r c)"), func=ACT.Square
+            out=sqd[:].rearrange("p v j c -> p (v j c)"), in_=sqd[:].rearrange("p v j c -> p (v j c)"), func=ACT.Square
+        )
+        nc.vector.tensor_reduce(out=r2c[:], in_=sqd[:], axis=mybir.AxisListType.X, op=ALU.add)
+        nc.sync.dma_start(
+            out=out_flat[TOK - BLOCKS : TOK, :].rearrange("k (s x) -> (k s) x", s=4),
+            in_=r2c[:].rearrange("p v j -> p (v j)"),
         )
 
         u_t = const.tile([P, 4, TOK], F32, name="u_t")
-        v_t = const.tile([P, 4, TOK], F32, name="v_t")
+        v_ps = {}
         hg = [const.tile([P, GROUPS, HALF, 4], BF16, name="hg%d" % q, align_bytes=64) for q in range(2)]
         hq = [const.tile([P, GROUPS * HALF], U32, name="hq%d" % q, align_bytes=64) for q in range(2)]
         hs = [const.tile([P, GROUPS * HALF], U8, name="hs%d" % q, align_bytes=64) for q in range(2)]
@@ -139,8 +139,11 @@ def tile_egnngatededgelayer_x2_kernel(
 
         uv_sb = {}
 
-        def project(q, n, copy):
+        accs = {}
+
+        def project(q, n):
             acc = bank("acc")
+            accs[q, n] = acc
             for g in range(GROUPS):
                 cols = slice(g * HALF, (g + 1) * HALF)
                 nc.tensor.matmul_mx(
@@ -152,37 +155,39 @@ def tile_egnngatededgelayer_x2_kernel(
                     start=(g == 0),
                     stop=(g == GROUPS - 1),
                 )
+
+        def take_uv(q, n, copy):
             uv = const.tile([P, 4, P], F32, name="uv%d%d" % (q, n))
             uv_sb[q, n] = uv
-            copy(out=uv[:], in_=acc[:].rearrange("q (p t) -> q t p", t=4))
+            copy(out=uv[:], in_=accs[q, n][:].rearrange("q (p t) -> q t p", t=4))
 
-        def turn_uv(q, n, copy):
-            uvt = bank("uvt")
+        def turn_uv(q, n, copy=None):
+            uvt = psum.tile([P, F], F32, name="v_ps", tag="v", bufs=2) if n else bank("uvt")
             for t in range(4):
                 nc.tensor.transpose(uvt[:, t * P : t * P + P], uv_sb[q, n][:, t, :], ident[:])
-            dst = v_t if n else u_t
-            copy(out=dst[:, :, q * HALF : (q + 1) * HALF], in_=uvt[:].rearrange("p (t r) -> p t r", t=4))
+            if n:
+                v_ps[q] = uvt
+            else:
+                copy(out=u_t[:, :, q * HALF : (q + 1) * HALF], in_=uvt[:].rearrange("p (t r) -> p t r", t=4))
 
         r2p = {}
 
         def spread_r2(k):
-            r2p[k] = psum.tile([P, ROWS], F32, name="r2p", tag="r2p", bufs=2)
-            for rt in range(TILES):
-                j = k * TILES + rt
-                nc.tensor.transpose(
-                    r2p[k][:, rt * P : rt * P + P], r2c[:, j : j + 1].to_broadcast([P, P]), ident[:]
-                )
+            r2p[k] = work.tile([P, ROWS], F32, name="r2p", bufs=5)
+            nc.sync.dma_start(out=r2p[k][:], in_=out_flat[TOK - BLOCKS + k, :].partition_broadcast(P))
 
+        for k in range(4):
+            spread_r2(k)
         turn_h(0, 0, nc.scalar.copy)
         turn_h(0, 1, nc.vector.tensor_copy)
         quant_h(0)
-        nc.vector.tensor_reduce(out=r2c[:], in_=sqd[:], axis=mybir.AxisListType.X, op=ALU.add)
         nc.vector.tensor_copy(out=wg[:, 0, :], in_=wr_raw[:])
         nc.vector.tensor_copy(out=wg[:, 1, :], in_=gain_raw[:])
-        project(0, 1, nc.scalar.copy)
-        spread_r2(0)
-        turn_uv(0, 1, nc.vector.tensor_copy)
-        project(0, 0, nc.scalar.copy)
+        project(0, 1)
+        project(0, 0)
+        take_uv(0, 1, nc.scalar.copy)
+        take_uv(0, 0, nc.vector.tensor_copy)
+        turn_uv(0, 1)
         turn_uv(0, 0, nc.scalar.copy)
 
         nc.gpsimd.tensor_copy(
@@ -210,32 +215,39 @@ def tile_egnngatededgelayer_x2_kernel(
                 out=pre[k][:, t, :].rearrange("p (i j) -> p i j", i=IB),
                 in0=r2p[k][:].rearrange("p (i j) -> p i j", i=IB),
                 scalar=wg[:, 0, t : t + 1],
-                in1=v_t[:, t, b * N : (b + 1) * N].unsqueeze(1).to_broadcast([P, IB, N]),
+                in1=v_ps[b // 2][:, t * P + b % 2 * N : t * P + b % 2 * N + N].unsqueeze(1).to_broadcast([P, IB, N]),
                 op0=ALU.mult,
                 op1=ALU.add,
             )
 
-        def edge_silu(k, t):
-            if t == 0:
+        def edge_silu(k, q):
+            if q == 0:
                 act[k] = work.tile([P, 4, ROWS], F32, name="act", bufs=4)
-            for i in range(IB):
-                tok = k * IB + i
-                nc.scalar.activation(
-                    out=act[k][:, t, i * N : i * N + N],
-                    in_=pre[k][:, t, i * N : i * N + N],
-                    func=ACT.Silu,
-                    bias=u_t[:, t, tok : tok + 1],
-                )
+            for t in range(4):
+                for i in (2 * q, 2 * q + 1):
+                    tok = k * IB + i
+                    nc.scalar.activation(
+                        out=act[k][:, t, i * N : i * N + N],
+                        in_=pre[k][:, t, i * N : i * N + N],
+                        func=ACT.Silu,
+                        bias=u_t[:, t, tok : tok + 1],
+                    )
 
         def edge_gain_mul(k, q):
             if q == 0:
                 abf[k] = work.tile([P, ROWS, 4], BF16, name="abf", align_bytes=64, bufs=4)
-            eng = nc.vector if k >= BLOCKS - 2 and q % 2 else nc.gpsimd
-            r0 = q * P
+            if k >= BLOCKS - 2:
+                eng, r0, n = (nc.vector if q % 2 else nc.gpsimd), q * P, P
+            elif k == 0:
+                eng, r0, n = nc.gpsimd, q * P, P
+            elif q % 2 == 1:
+                eng, r0, n = nc.gpsimd, (q - 1) * P, 2 * P
+            else:
+                return
             eng.tensor_tensor(
-                out=abf[k][:, r0 : r0 + P, :].rearrange("p (c i) t -> p c t i", i=4),
-                in0=act[k][:, :, r0 : r0 + P].rearrange("p t (c i) -> p c t i", i=4),
-                in1=wg[:, 1, :].unsqueeze(1).unsqueeze(3).to_broadcast([P, P // 4, 4, 4]),
+                out=abf[k][:, r0 : r0 + n, :].rearrange("p (c i) t -> p c t i", i=4),
+                in0=act[k][:, :, r0 : r0 + n].rearrange("p t (c i) -> p c t i", i=4),
+                in1=wg[:, 1, :].unsqueeze(1).unsqueeze(3).to_broadcast([P, n // 4, 4, 4]),
                 op=ALU.mult,
             )
 
@@ -293,7 +305,7 @@ def tile_egnngatededgelayer_x2_kernel(
                 )
 
         def wide(j):
-            return j % 5 in (1, 3) and j % 64 < 60
+            return j % 7 in (1, 3, 5) and j % 64 < 60
 
         outm = {}
 
@@ -367,52 +379,57 @@ def tile_egnngatededgelayer_x2_kernel(
                     out=out_2[0, 4 * s : 4 * s + 4, toks].bitcast(I32), in_=o_s[32 * s : 32 * s + 4, :].bitcast(I32)
                 )
             nc.sync.dma_start(
-                out=out_0.rearrange("b n f -> (b n) f")[toks, :], in_=o_t[:].rearrange("q p t -> q (p t)")
+                out=out_flat[toks, :], in_=o_t[:].rearrange("q p t -> q (p t)")
             )
 
         n_tiles = BLOCKS * TILES
+        half = n_tiles // 2
         late = {
             2: lambda: turn_h(1, 0, nc.vector.tensor_copy),
             4: lambda: turn_h(1, 1, nc.vector.tensor_copy),
             6: lambda: quant_h(1),
-            7: lambda: project(1, 1, nc.vector.tensor_copy),
-            9: lambda: turn_uv(1, 1, nc.vector.tensor_copy),
-            10: lambda: project(1, 0, nc.vector.tensor_copy),
+            7: lambda: project(1, 1),
+            8: lambda: project(1, 0),
+            9: lambda: take_uv(1, 1, nc.vector.tensor_copy),
+            10: lambda: take_uv(1, 0, nc.vector.tensor_copy),
+            11: lambda: turn_uv(1, 1),
             12: lambda: turn_uv(1, 0, nc.vector.tensor_copy),
         }
 
-        def go(idx, count, fn):
+        def go(idx, count, fn, *rest):
             if 0 <= idx < count:
-                fn(idx)
+                fn(idx, *rest)
 
-        for n in range(n_tiles + 26):
+        def go4(idx, fn):
+            if 0 <= idx < n_tiles:
+                fn(idx // 4, idx % 4)
+
+        for n in range(n_tiles + 24):
             k, q = divmod(n, 4)
-            half = n_tiles // 2
-            go(n - 15, n_tiles, msg_matmul)
+            go4(n - 6, edge_silu)
             go(n - 21, half, gather)
-            if n - 25 >= half:
-                go(n - 25, n_tiles, gather)
-            if q == 1:
-                go(k + 1, BLOCKS, spread_r2)
-            if k < BLOCKS:
-                edge_sum(k, q)
-            if 0 <= n - 3 < n_tiles:
-                edge_silu((n - 3) // 4, (n - 3) % 4)
-            if 0 <= n - 8 < n_tiles:
-                edge_gain_mul((n - 8) // 4, (n - 8) % 4)
+            if n - 23 >= half:
+                go(n - 23, n_tiles, gather)
             if q == 0:
-                go(k - 5, BLOCKS - 1, gate)
-            if n - 18 == n_tiles - 1 or n - 20 == n_tiles - 1:
-                gate(BLOCKS - 1, 0 if n - 18 == n_tiles - 1 else 2, 2 if n - 18 == n_tiles - 1 else 4)
-            go(n - 15, n_tiles, msg_silu)
+                go(k + 4, BLOCKS, spread_r2)
+            go4(n, edge_sum)
             if q == 1:
                 go(k - 3, BLOCKS, edge_quant)
+            go(n - 14, n_tiles, msg_matmul)
+            if q == 3:
+                go(k - 4, BLOCKS - 1, gate)
+            if n - 17 == n_tiles - 1:
+                gate(BLOCKS - 1, 0, 2)
+            if n - 19 == n_tiles - 1:
+                gate(BLOCKS - 1, 2, 4)
+            go(n - 14, n_tiles, msg_silu)
+            go4(n - 8, edge_gain_mul)
             go(n - 15, n_tiles, msg_gate)
             if n in late:
                 late[n]()
-            if n - 23 == half - 1:
+            if n - 22 == half - 1:
                 take_sums(0)
-            if n - 29 == half - 1:
+            if n - 28 == half - 1:
                 finish(0)
         take_sums(1)
         finish(1)

from contextlib import ExitStack

import concourse.mybir as mybir
from concourse.masks import make_identity

F32 = mybir.dt.float32
BF16 = mybir.dt.bfloat16
I32 = mybir.dt.int32
U32 = mybir.dt.uint32
U8 = mybir.dt.uint8
FP8X4 = mybir.dt.float8_e4m3fn_x4
FP4X4 = mybir.dt.float4_e2m1fn_x4
ACT = mybir.ActivationFunctionType
ALU = mybir.AluOpType

P = 128
B, N, D, F = 4, 64, 2048, 512
GROUPS = D // 512
TOK = B * N
HALF = 128
IB = 8
ROWS = IB * N
BLOCKS = TOK // IB
TILES = ROWS // P
FLOPS = 2 * TOK * D * 2 * F + 2 * B * N * N * F * F


def tile_egnngatededgelayer_x2_kernel(
    tc, h, pos, w1_words, w1_scales, wr, edge_gain, w2_words, w2_scales, gate_w, out_0, out_1, out_2
):
    nc = tc.nc
    with ExitStack() as ctx:
        const = ctx.enter_context(tc.tile_pool(name="const", bufs=1))
        work = ctx.enter_context(tc.tile_pool(name="work", bufs=3))
        msgs = ctx.enter_context(tc.tile_pool(name="msgs", bufs=18))
        psum = ctx.enter_context(tc.psum_pool(name="psum", bufs=1))
        ctx.enter_context(tc.manual_schedule())

        def bank(name):
            return psum.tile([P, 512], F32, name=name, tag="mm", bufs=3)

        w1s = const.tile([P, GROUPS, 2 * F], U8, name="w1s", align_bytes=64)
        w1s_i = w1s[:].rearrange("p g n -> p (g n)").bitcast(I32).rearrange("p (g n) -> p g n", g=GROUPS)
        w2s_raw = const.tile([P, F], U8, name="w2s_raw", align_bytes=64)
        pos_i = const.tile([P, 2, 3], BF16, name="pos_i")
        pos_j = const.tile([P, N, 3], BF16, name="pos_j")
        gms = [const.tile([P, TILES, 2 * P], F32, name="gm%d" % q) for q in range(4)]
        zero = const.tile([P, P], F32, name="zero")
        gate_row = const.tile([P, F], BF16, name="gate_row")
        gate_perm = const.tile([P, F], BF16, name="gate_perm")
        ones = const.tile([P, P], BF16, name="ones")
        ident = const.tile([P, P], F32, name="ident")
        mask = const.tile([P, 2], F32, name="mask")
        wr_raw = const.tile([P, 4], BF16, name="wr_raw")
        gain_raw = const.tile([P, 4], BF16, name="gain_raw")
        wg = const.tile([P, 2, 4], F32, name="wg")

        nc.vector.memset(w1s[:].rearrange("p g n -> p (g n)").bitcast(I32), 0)
        make_identity(nc, ident[:])
        nc.gpsimd.memset(ones[:], 1.0)
        nc.gpsimd.memset(gate_row[:], 0.0)
        nc.gpsimd.memset(w2s_raw[:].bitcast(I32), 0)
        nc.gpsimd.memset(zero[:], 0.0)
        for q in range(4):
            nc.gpsimd.memset(gms[q][:], 0.0)
        for s in range(2):
            for v in range(2):
                nc.gpsimd.memset(mask[64 * v : 64 * v + 64, s : s + 1], 0.0625 if s == v else 0.0)

        h_flat = h.rearrange("b n d -> (b n) d")
        h_sb = [const.tile([P, D], BF16, name="h_sb%d" % q) for q in range(2)]
        w1t = const.tile([P, GROUPS, 4 * F], U8, name="w1t", align_bytes=64)
        w1t_i = w1t[:].rearrange("p g n -> p (g n)").bitcast(I32).rearrange("p (g n) -> p g n", g=GROUPS)
        w1_i = w1_words.bitcast(I32).rearrange("g p n -> p g n")
        w1s_hbm = w1_scales.bitcast(I32).rearrange("g r n -> r g n")
        w2_raw = const.tile([P, 2 * F], U8, name="w2_raw", align_bytes=64)

        nc.scalar.dma_start(out=pos_i[:], in_=pos.rearrange("b (i v) c -> (b i) v c", v=2))
        for b in range(B):
            nc.scalar.dma_start(
                out=pos_j[32 * b : 32 * b + 32].rearrange("p j c -> p (j c)"),
                in_=pos[b].rearrange("j c -> (j c)").partition_broadcast(32),
            )
        for q in range(2):
            nc.sync.dma_start(out=h_sb[0][:, q * 1024 : q * 1024 + 1024], in_=h_flat[0:HALF, q * 1024 : q * 1024 + 1024])
        for q in range(4):
            nc.sync.dma_start(out=w1s_i[32 * q : 32 * q + 4], in_=w1s_hbm[4 * q : 4 * q + 4])
        for n in (1, 0):
            nc.sync.dma_start(out=w1t_i[:, :, n * 256 : n * 256 + 256], in_=w1_i[:, :, n * 256 : n * 256 + 256])
        nc.scalar.dma_start(out=wr_raw[:], in_=wr.rearrange("(p t) -> p t", t=4))
        nc.scalar.dma_start(out=gain_raw[:], in_=edge_gain.rearrange("(p t) -> p t", t=4))
        nc.scalar.dma_start(out=gate_row[0:1, :], in_=gate_w.unsqueeze(0))
        nc.sync.dma_start(out=w2_raw[:].bitcast(I32), in_=w2_words[0].bitcast(I32))
        for q in range(4):
            nc.sync.dma_start(
                out=w2s_raw[32 * q : 32 * q + 4, :].bitcast(I32), in_=w2_scales[0, 4 * q : 4 * q + 4, :].bitcast(I32)
            )
        nc.sync.dma_start(out=h_sb[1][:], in_=h_flat[HALF:TOK, :])

        sqd = const.tile([P, 2, N, 3], F32, name="sqd")
        r2c = const.tile([P, 2, N], F32, name="r2c")
        out_flat = out_0.rearrange("b n f -> (b n) f")
        nc.vector.tensor_tensor(
            out=sqd[:],
            in0=pos_j[:].unsqueeze(1).to_broadcast([P, 2, N, 3]),
            in1=pos_i[:].unsqueeze(2).to_broadcast([P, 2, N, 3]),
            op=ALU.subtract,
        )
        nc.scalar.activation(
            out=sqd[:].rearrange("p v j c -> p (v j c)"), in_=sqd[:].rearrange("p v j c -> p (v j c)"), func=ACT.Square
        )
        nc.vector.tensor_reduce(out=r2c[:], in_=sqd[:], axis=mybir.AxisListType.X, op=ALU.add)
        nc.sync.dma_start(
            out=out_flat[TOK - BLOCKS : TOK, :].rearrange("k (s x) -> (k s) x", s=4),
            in_=r2c[:].rearrange("p v j -> p (v j)"),
        )

        u_t = const.tile([P, 4, TOK], F32, name="u_t")
        v_ps = {}
        hg = [const.tile([P, GROUPS, HALF, 4], BF16, name="hg%d" % q, align_bytes=64) for q in range(2)]
        hq = [const.tile([P, GROUPS * HALF], U32, name="hq%d" % q, align_bytes=64) for q in range(2)]
        hs = [const.tile([P, GROUPS * HALF], U8, name="hs%d" % q, align_bytes=64) for q in range(2)]

        def turn_h(q, pair, copy):
            words = h_sb[q][:].bitcast(F32)
            xt = bank("xt")
            xv = xt[:].rearrange("p (g u r) -> p g u r", g=2, u=2)
            for gg in range(2):
                g = 2 * pair + gg
                for u in range(2):
                    nc.tensor.transpose(xv[:, gg, u, :], words[:, 256 * g + u : 256 * (g + 1) : 2], ident[:])
            dst = hg[q][:].rearrange("p g r t -> p (g r t)").bitcast(F32).rearrange("p (g r u) -> p g r u", g=GROUPS, u=2)
            copy(out=dst[:, 2 * pair : 2 * pair + 2], in_=xv.rearrange("p g u r -> p g r u"))

        def quant_h(q):
            nc.vector.quantize_mx(
                out=hq[q][:].bitcast(FP8X4), scales=hs[q][:], in_=hg[q][:].rearrange("p g r t -> p (g r t)")
            )

        uv_sb = {}

        accs = {}

        def project(q, n):
            acc = bank("acc")
            accs[q, n] = acc
            for g in range(GROUPS):
                cols = slice(g * HALF, (g + 1) * HALF)
                nc.tensor.matmul_mx(
                    out=acc[:],
                    lhsT=hq[q][:, cols].bitcast(FP8X4),
                    lhsT_scale=hs[q][:, cols],
                    rhs=w1t[:, g, n * 1024 : n * 1024 + 1024].bitcast(FP4X4),
                    rhs_scale=w1s[:, g, n * 512 : n * 512 + 512],
                    start=(g == 0),
                    stop=(g == GROUPS - 1),
                )

        def take_uv(q, n, copy):
            uv = const.tile([P, 4, P], F32, name="uv%d%d" % (q, n))
            uv_sb[q, n] = uv
            copy(out=uv[:], in_=accs[q, n][:].rearrange("q (p t) -> q t p", t=4))

        def turn_uv(q, n, copy=None):
            uvt = psum.tile([P, F], F32, name="v_ps", tag="v", bufs=2) if n else bank("uvt")
            for t in range(4):
                nc.tensor.transpose(uvt[:, t * P : t * P + P], uv_sb[q, n][:, t, :], ident[:])
            if n:
                v_ps[q] = uvt
            else:
                copy(out=u_t[:, :, q * HALF : (q + 1) * HALF], in_=uvt[:].rearrange("p (t r) -> p t r", t=4))

        r2p = {}

        def spread_r2(k):
            r2p[k] = work.tile([P, ROWS], F32, name="r2p", bufs=5)
            nc.sync.dma_start(out=r2p[k][:], in_=out_flat[TOK - BLOCKS + k, :].partition_broadcast(P))

        for k in range(4):
            spread_r2(k)
        turn_h(0, 0, nc.scalar.copy)
        turn_h(0, 1, nc.vector.tensor_copy)
        quant_h(0)
        nc.vector.tensor_copy(out=wg[:, 0, :], in_=wr_raw[:])
        nc.vector.tensor_copy(out=wg[:, 1, :], in_=gain_raw[:])
        project(0, 1)
        project(0, 0)
        take_uv(0, 1, nc.scalar.copy)
        take_uv(0, 0, nc.vector.tensor_copy)
        turn_uv(0, 1)
        turn_uv(0, 0, nc.scalar.copy)

        nc.gpsimd.tensor_copy(
            out=gate_perm[:].rearrange("k (t p) -> k t p", t=4), in_=gate_row[:].rearrange("k (p t) -> k t p", t=4)
        )
        gw = psum.tile([P, F], F32, name="gw", tag="gw", bufs=1)
        nc.tensor.matmul(gw[:], ones[:], gate_perm[:], start=True, stop=True)
        w2p = const.tile([P, 2 * F], U8, name="w2p", align_bytes=64)
        w2sp = const.tile([P, F], U8, name="w2sp", align_bytes=64)
        nc.gpsimd.tensor_copy(
            out=w2p[:].rearrange("k (t p w) -> k p t w", t=4, w=2), in_=w2_raw[:].rearrange("k (p t w) -> k p t w", t=4, w=2)
        )
        nc.gpsimd.tensor_copy(
            out=w2sp[:].rearrange("k (t p) -> k p t", t=4), in_=w2s_raw[:].rearrange("k (p t) -> k p t", t=4)
        )

        pre, act, abf, aq, asc, yb, mt, gp, gm = {}, {}, {}, {}, {}, {}, {}, {}, {}
        outp = {}

        def edge_sum(k, t):
            b = k // (N // IB)
            if t == 0:
                pre[k] = work.tile([P, 4, ROWS], F32, name="pre")
            nc.vector.scalar_tensor_tensor(
                out=pre[k][:, t, :].rearrange("p (i j) -> p i j", i=IB),
                in0=r2p[k][:].rearrange("p (i j) -> p i j", i=IB),
                scalar=wg[:, 0, t : t + 1],
                in1=v_ps[b // 2][:, t * P + b % 2 * N : t * P + b % 2 * N + N].unsqueeze(1).to_broadcast([P, IB, N]),
                op0=ALU.mult,
                op1=ALU.add,
            )

        def edge_silu(k, q):
            if q == 0:
                act[k] = work.tile([P, 4, ROWS], F32, name="act", bufs=4)
            for t in range(4):
                for i in (2 * q, 2 * q + 1):
                    tok = k * IB + i
                    nc.scalar.activation(
                        out=act[k][:, t, i * N : i * N + N],
                        in_=pre[k][:, t, i * N : i * N + N],
                        func=ACT.Silu,
                        bias=u_t[:, t, tok : tok + 1],
                    )

        def edge_gain_mul(k, q):
            if q == 0:
                abf[k] = work.tile([P, ROWS, 4], BF16, name="abf", align_bytes=64, bufs=4)
            if k >= BLOCKS - 2:
                eng, r0, n = (nc.vector if q % 2 else nc.gpsimd), q * P, P
            elif k == 0:
                eng, r0, n = nc.gpsimd, q * P, P
            elif q % 2 == 1:
                eng, r0, n = nc.gpsimd, (q - 1) * P, 2 * P
            else:
                return
            eng.tensor_tensor(
                out=abf[k][:, r0 : r0 + n, :].rearrange("p (c i) t -> p c t i", i=4),
                in0=act[k][:, :, r0 : r0 + n].rearrange("p t (c i) -> p c t i", i=4),
                in1=wg[:, 1, :].unsqueeze(1).unsqueeze(3).to_broadcast([P, n // 4, 4, 4]),
                op=ALU.mult,
            )

        def edge_quant(k):
            aq[k] = work.tile([P, ROWS], U32, name="aq", align_bytes=64, bufs=4)
            asc[k] = work.tile([P, ROWS], U8, name="asc", align_bytes=64, bufs=4)
            nc.vector.quantize_mx(
                out=aq[k][:].bitcast(FP8X4), scales=asc[k][:], in_=abf[k][:].rearrange("p r t -> p (r t)")
            )

        def msg_matmul(j):
            k, rt = divmod(j, TILES)
            cols = slice(rt * P, rt * P + P)
            yb[j] = bank("y")
            nc.tensor.matmul_mx(
                out=yb[j][:],
                lhsT=aq[k][:, cols].bitcast(FP8X4),
                lhsT_scale=asc[k][:, cols],
                rhs=w2p[:].bitcast(FP4X4),
                rhs_scale=w2sp[:],
                start=True,
                stop=True,
            )

        def msg_silu(j):
            mt[j] = msgs.tile([P, F], F32, name="mt")
            nc.scalar.activation(out=mt[j][:], in_=yb[j][:], func=ACT.Silu)

        def msg_gate(j):
            k, rt = divmod(j, TILES)
            if rt == 0:
                gp[k] = work.tile([P, TILES], F32, name="gp")
            prod = work.tile([P, F], F32, name="prod")
            nc.vector.scalar_tensor_tensor(
                out=prod[:],
                in0=mt[j][:],
                scalar=1.0,
                in1=gw[:],
                op0=ALU.mult,
                op1=ALU.mult,
                accum_out=gp[k][:, rt : rt + 1],
            )

        def gate(k, lo=0, hi=TILES):
            th = work.tile([P, TILES], F32, name="th")
            gm[k] = gms[k % 4]
            nc.scalar.activation(out=th[:, lo:hi], in_=gp[k][:, lo:hi], func=ACT.Tanh, scale=0.5)
            for s in range(2):
                nc.scalar.activation(
                    out=gm[k][:, lo:hi, 126 + s],
                    in_=th[:, lo:hi],
                    func=ACT.Identity,
                    scale=mask[:, s : s + 1],
                    bias=mask[:, s : s + 1],
                )

        def wide(j):
            return j % 7 in (1, 3, 5) and j % 64 < 60

        outm = {}

        def gather(j):
            k, rt = divmod(j, TILES)
            q, col = divmod(2 * j, HALF)
            if col == 0:
                outp[q] = psum.tile([P, 4, HALF], F32, name="outp", tag="outp", bufs=1)
                outm[q] = psum.tile([P, F], F32, name="outm", tag="outm", bufs=1)
                for t in range(4):
                    nc.tensor.transpose(outp[q][:, t, :], zero[:], ident[:])
            wides = [x for x in range(q * 64, q * 64 + 64) if wide(x)]
            if wide(j):
                nc.tensor.matmul(
                    outm[q][:],
                    gm[k][:, rt, 126 - col : 254 - col],
                    mt[j][:],
                    start=(j == wides[0]),
                    stop=(j == wides[-1]),
                )
            else:
                for t in range(4):
                    nc.tensor.matmul(
                        outp[q][:, t, col : col + 2],
                        mt[j][:, t * P : t * P + P],
                        gm[k][:, rt, 126:128],
                        start=True,
                        stop=True,
                    )

        sums = {}

        def take_sums(q):
            o_m = const.tile([P, F], F32, name="o_m%d" % q)
            o_p = const.tile([P, 4, HALF], F32, name="o_p%d" % q)
            nc.vector.tensor_copy(out=o_m[:], in_=outm[q][:])
            nc.scalar.copy(out=o_p[:], in_=outp[q][:])
            sums[q] = (o_m, o_p)

        def finish(q):
            o_m, o_p = sums[q]
            o_bf = const.tile([P, HALF, 4], BF16, name="o_bf%d" % q, align_bytes=64)
            o_q = const.tile([P, HALF], U32, name="o_q%d" % q, align_bytes=64)
            o_s = const.tile([P, HALF], U8, name="o_s%d" % q, align_bytes=64)
            o_t = const.tile([P, P, 4], F32, name="o_t%d" % q)
            pl = bank("pl")
            for t in range(4):
                nc.tensor.transpose(pl[:, t * P : t * P + P], o_m[:, t * P : t * P + P], ident[:])
            ob = bank("ob")
            for t in range(4):
                nc.tensor.transpose(ob[:, t * P : t * P + P], o_p[:, t, :], ident[:])
            nc.vector.tensor_tensor(
                out=o_bf[:],
                in0=pl[:].rearrange("p (t r) -> p r t", t=4),
                in1=o_p[:].rearrange("p t r -> p r t"),
                op=ALU.add,
            )
            nc.vector.tensor_tensor(
                out=o_t[:],
                in0=ob[:].rearrange("q (t p) -> q p t", t=4),
                in1=o_m[:].rearrange("q (t p) -> q p t", t=4),
                op=ALU.add,
            )
            nc.vector.quantize_mx(out=o_q[:].bitcast(FP8X4), scales=o_s[:], in_=o_bf[:].rearrange("p r t -> p (r t)"))
            toks = slice(q * HALF, (q + 1) * HALF)
            nc.sync.dma_start(
                out=out_1[0].rearrange("p m t -> p (m t)")[:, q * 512 : q * 512 + 512].bitcast(I32), in_=o_q[:].bitcast(I32)
            )
            for s in range(4):
                nc.sync.dma_start(
                    out=out_2[0, 4 * s : 4 * s + 4, toks].bitcast(I32), in_=o_s[32 * s : 32 * s + 4, :].bitcast(I32)
                )
            nc.sync.dma_start(
                out=out_flat[toks, :], in_=o_t[:].rearrange("q p t -> q (p t)")
            )

        n_tiles = BLOCKS * TILES
        half = n_tiles // 2
        late = {
            2: lambda: turn_h(1, 0, nc.vector.tensor_copy),
            4: lambda: turn_h(1, 1, nc.vector.tensor_copy),
            6: lambda: quant_h(1),
            7: lambda: project(1, 1),
            8: lambda: project(1, 0),
            9: lambda: take_uv(1, 1, nc.vector.tensor_copy),
            10: lambda: take_uv(1, 0, nc.vector.tensor_copy),
            11: lambda: turn_uv(1, 1),
            12: lambda: turn_uv(1, 0, nc.vector.tensor_copy),
        }

        def go(idx, count, fn, *rest):
            if 0 <= idx < count:
                fn(idx, *rest)

        def go4(idx, fn):
            if 0 <= idx < n_tiles:
                fn(idx // 4, idx % 4)

        for n in range(n_tiles + 24):
            k, q = divmod(n, 4)
            go4(n - 6, edge_silu)
            go(n - 21, half, gather)
            if n - 23 >= half:
                go(n - 23, n_tiles, gather)
            if q == 0:
                go(k + 4, BLOCKS, spread_r2)
            go4(n, edge_sum)
            if q == 1:
                go(k - 3, BLOCKS, edge_quant)
            go(n - 14, n_tiles, msg_matmul)
            if q == 3:
                go(k - 4, BLOCKS - 1, gate)
            if n - 17 == n_tiles - 1:
                gate(BLOCKS - 1, 0, 2)
            if n - 19 == n_tiles - 1:
                gate(BLOCKS - 1, 2, 4)
            go(n - 14, n_tiles, msg_silu)
            go4(n - 8, edge_gain_mul)
            go(n - 15, n_tiles, msg_gate)
            if n in late:
                late[n]()
            if n - 22 == half - 1:
                take_sums(0)
            if n - 28 == half - 1:
                finish(0)
        take_sums(1)
        finish(1)
